import numpy as np, ml_dtypes
CORES = [3,7,11,15,131,135,139,143]
N = 8
import mx_ref
BF = ml_dtypes.bfloat16
def entries(a):
    return np.ascontiguousarray(a.T).reshape(-1)
def table(e):
    return np.ascontiguousarray(np.reshape(e, (-1, 16)).T).astype(np.int32)
def cols(t, e):
    v = np.concatenate([t.reshape(128, -1, 4), np.zeros((128, 1, 4), BF)], axis=1)
    return np.ascontiguousarray(v[:, e]).reshape(128, -1)
def f(rng, *shape):
    return mx_ref.flush((rng.standard_normal(shape, dtype=np.float32) * np.exp2(rng.integers(-2, 3, shape[:-1] + (1,)))).astype(BF))
def wide(rng, *shape, cols=0):
    v = rng.standard_normal(shape, dtype=np.float32) * np.exp2(rng.integers(-12, 13, shape)).astype(np.float32)
    if cols: v *= np.repeat(np.exp2(rng.integers(-cols, cols + 1, shape[:-2] + (1, shape[-1] // 4))) * (rng.random(shape[:-2] + (1, shape[-1] // 4)) > 0.0625), 4, axis=-1).astype(np.float32)
    return mx_ref.flush(v.astype(BF))
B, K, O = 192, 64, 3
def order(r):
    return list(range(r + 1))
def some(rng, where, n):
    e = np.full(K, -1); e[rng.permutation(K)[:n]] = rng.permutation(where)[:n]
    return table(e)
def setup_inputs(rng):
    return {"b": f(rng, N, 128, 4 * B), "x": f(rng, N, 128, 4 * K), "w": f(rng, N, 128, 512 * O), "pl": np.stack([some(rng, np.arange(B), int(rng.integers(K >> 1, K + 1))) for r in range(N)])}
def setup_inputs_same(rng):
    d = setup_inputs(rng)
    for i in range(50):
        at = rng.permutation(B)[:K]; quiet = rng.permutation(N)[:int(rng.integers(1, 3))].tolist()
        pl = [some(rng, at, 0 if r in quiet else int(rng.integers(K >> 2, (3 * K >> 2) + 1))) for r in range(N)]
        s = [set(entries(pl[r]).tolist()) - {-1} for r in range(N) if r not in quiet]
        if all(s[j] & s[k] for j in range(len(s)) for k in range(j)):
            d["pl"] = np.stack(pl); return d
    raise RuntimeError("no draw in which any two of the writing ranks have a place in common")
def setup_inputs_apart(rng):
    d = setup_inputs(rng); at, start = rng.permutation(B), 0
    pl = [None] * N
    for i in range(N):
        e = at[K * i:K * i + K]
        pl[(start + i) % N] = some(rng, e, len(e))
    d["pl"] = np.stack(pl); return d
def setup_inputs_runs(rng):
    d = setup_inputs(rng); p = rng.permutation(N)
    pl = [None] * N
    for i in range(N):
        if i == 0: at = np.arange(0)
        elif i % 3 == 1: at = (int(rng.integers(B)) + np.arange(K)) % B
        elif i % 3 == 2: at = np.flatnonzero(np.isin(np.arange(B) % 8, rng.permutation(8)[:8 * K // B]))
        else: at = rng.permutation(B)[:K - int(rng.integers(K >> 2, (3 * K >> 2) + 1))]
        at = rng.permutation(at); a = int(rng.integers(len(at) + 1))
        pl[p[i]] = table(np.concatenate([at[:a], np.full(K - len(at), -1), at[a:]]))
    d["pl"] = np.stack(pl); return d
def setup_inputs_halves(rng):
    d = setup_inputs(rng); at, start = rng.permutation(B), 0
    pl = [None] * N
    for i in range(N): pl[(start + i) % N] = some(rng, at[:B >> 1] if i < N >> 1 else at[B >> 1:], K)
    d["pl"] = np.stack(pl); return d
def setup_inputs_spread(rng):
    d = setup_inputs(rng); d["b"] = wide(rng, N, 128, 4 * B, cols=6); d["x"] = wide(rng, N, 128, 4 * K, cols=6); return d
def check_inputs(d):
    bad = []
    for r in range(N):
        e = entries(d["pl"][r])
        if e.min() < -1 or e.max() >= B: bad.append("pl")
        e = e[e >= 0]
        if len(set(e.tolist())) != len(e): bad.append("pl names a place twice")
    return bad
def reference(b, x, w, pl):
    y = np.zeros((N, 128, O * B), np.float32)
    for r in range(N):
        m = np.array(b[r]).reshape(128, B, 4)
        for s in order(r):
            e = entries(pl[s]); k = np.flatnonzero(e >= 0)
            m[:, e[k]] = x[s].reshape(128, K, 4)[:, k]
        q = mx_ref.quantize(m.reshape(128, 4 * B))
        for o in range(O):
            y[r][:, B * o:B * o + B] = mx_ref.matmul(mx_ref.quantize(cols(w[r], np.arange(128 * o, 128 * o + 128))), q)
    return {"y": y}

@@ -1,0 +1,293 @@
+from concourse.bass import DstId, RemoteDMATransfer
+from concourse.mybir import dt, AluOpType, ActivationFunctionType
+
+B, K, O, N = 192, 64, 3, 8
+LEAD = 16
+STEP = K
+PL = LEAD + B + LEAD
+W0 = STEP * LEAD
+TAB = STEP * PL + 1
+NB = B // 32
+WIN = B + K * (N + 1)
+SCRATCH = {
+    "xt": ("sbuf", [128, 8 * K], "bfloat16"),
+    "bt": ("sbuf", [128, 4 * B], "bfloat16"),
+    "wt": ("sbuf", [128, 512 * O], "bfloat16"),
+    "win": ("sbuf", [128, WIN], "float8_e4m3fn_x4"),
+    "pln": ("sbuf", [128, WIN], "uint8"),
+    "wq": ("sbuf", [128, 128 * O], "float8_e4m3fn_x4"),
+    "wp": ("sbuf", [128, 128 * O], "uint8"),
+    "mq": ("sbuf", [128, B], "float8_e4m3fn_x4"),
+    "mp": ("sbuf", [128, B], "uint8"),
+    "ysb": ("sbuf", [128, O * B], "float32"),
+    "acc": ("psum", [128, 512 * O], "float32"),
+    "L": ("dram", [N, 128, 1], "int32"),
+    "li": ("sbuf", [128, 4], "int32"),
+    "lf": ("sbuf", [128, 4], "float32"),
+    "lo": ("sbuf", [128, 4], "uint16"),
+    "sp": ("sbuf", [128, 4], "int32"),
+    "sp2": ("sbuf", [128, 4], "int32"),
+    "gap": ("sbuf", [128, 4], "float32"),
+    "pg": ("sbuf", [128, 1], "int32"),
+    "slot": ("sbuf", [128, 1], "float32"),
+    "jb": ("sbuf", [128, 1], "int32"),
+    "jo": ("sbuf", [128, 1], "int32"),
+    "jp": ("sbuf", [128, 1], "int32"),
+    "jx": ("sbuf", [128, 1], "int32"),
+    "jt": ("sbuf", [128, 1], "int32"),
+    "jm": ("sbuf", [128, 1], "int32"),
+    "js": ("sbuf", [128, 1], "int32"),
+    "sel": ("sbuf", [128, 2], "uint16"),
+    "val": ("sbuf", [128, K], "float32"),
+    "tb": ("sbuf", [128, TAB], "float32"),
+    "tt": ("sbuf", [128, 32 * (2 * NB + 1)], "float32"),
+    "ee": ("sbuf", [128, 2 * NB + 1], "float32"),
+    "u2": ("sbuf", [64, 2 * NB + 1], "float32"),
+    "u3": ("sbuf", [128, 2 * NB + 1], "float32"),
+    "off": ("sbuf", [128, 16], "uint16"),
+}
+SEMAPHORES = ["lx", "lp", "lb", "lw", "lw2", "ll", "sy0", "sy1", "sy2", "lm", "it", "vv", "qx", "qb", "qw", "qw2", "of",
+              "pk", "ps", "mm0", "mm1", "mm2", "yc0", "yc1", "yc2", "go", "sent", "ls", "f0c", "f1c", "fp", "rc", "rp"]
+
+
+def bits(es):
+    m = 0
+    for e in es:
+        m |= 1 << e
+    return m
+
+
+def plan(T, topo):
+    C = T.cores
+    low = topo.host(C[0])
+    chips = []
+    for r in range(N):
+        if chips and C[r] in topo.cores_of(C[chips[-1][0]]):
+            chips[-1].append(r)
+        else:
+            chips.append([r])
+    home = [c for c in chips if topo.host(C[c[0]]) == low]
+    away = [c for c in chips if c not in home]
+    calls, lists = {}, {}
+    for s in range(N):
+        mine = [c for c in chips if s in c][0]
+        far = [r for r in range(N) if r not in mine]
+        out = topo.engines(C[s], C[far[0]])
+        mate = [r for r in mine if r != s][0]
+        stay = [e for e in topo.engines(C[s], C[mate]) if e not in out]
+        near = [r for r in far if r > s and topo.host(C[r]) == topo.host(C[s])]
+        up = [mate] if mate > s else []
+        if s < N - 1:
+            lists[s] = (out[:1], list(range(N - 1, s, -1)))
+        calls[s] = []
+
+        def slot(parts):
+            for what in ("c", "p"):
+                calls[s].append((s, 1, what, [], [(es, rs, sem[what]) for es, rs, sem in parts]))
+
+        rsem = {"c": "rc", "p": "rp"}
+        if mine in home:
+            cross = sorted([c[0] for c in away], key=lambda r: not topo.same_plane(C[s], C[r]))
+            slot([(out, cross, {"c": "f%dc" % home.index(mine), "p": "fp"})])
+            if near:
+                slot([(out, near, rsem)] + ([(stay[:4], up, rsem)] if up else []))
+            elif up:
+                slot([(out, up, rsem)])
+        else:
+            if near:
+                slot([(out, near, rsem)] + ([(stay, up, rsem)] if up else []))
+            elif up:
+                slot([(out + stay, up, rsem)])
+            if up:
+                for c in sorted(home, key=lambda c: not topo.same_plane(C[s], C[c[0]])):
+                    calls[s].append((c[0], len(c), "c", ["f%dc" % home.index(c)], [(out + stay, up, "rc")]))
+                calls[s].append((home[0][0], sum(len(c) for c in home), "p", ["fp"], [(out + stay, up, "rp")]))
+    want = {r: {} for r in range(N)}
+    for s in range(N):
+        for _, _, _, _, tr in calls[s]:
+            for es, rs, sem in tr:
+                for r in rs:
+                    want[r][sem] = want[r].get(sem, 0) + len(es)
+    return calls, lists, want, low
+
+
+def rank_program(g, core, T, topo):
+    rank = T.rank_of(core)
+    if rank is None:
+        return
+    C = T.cores
+    calls, nlist, wants, low = plan(T, topo)
+    want = wants[rank]
+    first = topo.host(core) == low
+    S = T.sem
+    op = AluOpType
+    Copy = ActivationFunctionType.Copy
+    a = B + K * rank
+    full = B + K * (rank + 1)
+    lists = sum(len(nlist[s][0]) for s in nlist if rank in nlist[s][1])
+
+    def dst(r):
+        rid, pid = topo.addr(C[r], core)
+        return DstId(rid=rid, pnc=pid)
+
+    g.scalar.dma_start(T.L[rank, 0:K, :], T.pl[:]).then_inc(S.lp, 16)
+    g.sync.dma_start(T.L[rank, K:2 * K, :], T.pl[:]).then_inc(S.lp, 16)
+    g.sync.dma_start(T.xt[:, 0:4 * K], T.x[:]).then_inc(S.lx, 16)
+    g.scalar.dma_start(T.bt[:], T.b[:]).then_inc(S.lb, 16)
+    g.scalar.dma_start(T.wt[:, 0:1024], T.w[:, 0:1024]).then_inc(S.lw, 16)
+    if first:
+        g.scalar.wait_ge(S.go, 1)
+    g.scalar.dma_start(T.wt[:, 1024:1536], T.w[:, 1024:1536]).then_inc(S.lw2, 16)
+
+    g.iota(T.sp[:], [[16, 4]], 0, 1).then_inc(S.it, 1)
+    sent = 0
+    if rank in nlist:
+        es, rs = nlist[rank]
+        g.wait_ge(S.lp, 32)
+        g.remote_dma_fused([RemoteDMATransfer(dst_ids=[dst(r) for r in rs], dma_engine_mask=bits(es), remote_sem=S.ls,
+                                              srcs=[T.L[rank]], dsts=[T.L[rank] for r in rs])], local_sem=S.sent)
+        sent += len(es)
+    ready = False
+    for slot, n, what, waits, tr in calls[rank]:
+        c0, c1 = B + K * slot, B + K * (slot + n)
+        if slot == rank and not ready:
+            g.wait_ge(S.qx, 1)
+            ready = True
+        for w in waits:
+            g.wait_ge(S[w], want[w])
+        view = T.win[:, c0:c1].bitcast(dt.uint8) if what == "c" else T.pln[:, c0:c1]
+        ts = [RemoteDMATransfer(dst_ids=[dst(r) for r in rs], dma_engine_mask=bits(es), remote_sem=S[sem],
+                                srcs=[view], dsts=[view for r in rs]) for es, rs, sem in tr]
+        g.remote_dma_fused(ts, local_sem=S.sent)
+        sent += sum(len(es) for es, rs, sem in tr)
+    if first:
+        g.sem_inc(S.go, 1)
+    if sent:
+        g.wait_ge(S.sent, sent)
+
+    nv = [0]
+
+    def V(ins):
+        ins.then_inc(S.vv, 1)
+        nv[0] += 1
+
+    def sync():
+        g.vector.wait_ge(S.vv, nv[0])
+
+    def places(l0, l1):
+        return T.tb[:, W0 + STEP * (l0 + 1):W0 + STEP * l1 + 1:STEP]
+
+    v = g.vector
+    V(v.memset(T.xt[:, 4 * K:8 * K], 0.0))
+    v.memset(T.li[:], -1).then_inc(S.lm, 1)
+    V(v.memset(T.tt[:, 0:PL], 1.0))
+    sync()
+    V(v.tensor_tensor_scan(places(-LEAD, B + LEAD), T.tt[:, 0:PL], T.tt[:, 0:PL], float(-LEAD - 1), op.add, op.mult))
+    v.wait_ge(S.lx, 16)
+    v.quantize_mx(T.win[:, a:a + 2 * K], T.pln[:, a:a + 2 * K], T.xt[:]).then_inc(S.qx, 1)
+    v.wait_ge(S.it, 1)
+    V(v.tensor_scalar(T.sp2[:], T.sp[:], K - 1, None, op.bitwise_and))
+    V(v.tensor_scalar(T.pg[:], T.sp[:, 0:1], 112, None, op.bitwise_and))
+    V(v.tensor_scalar(T.jb[:], T.sp[:, 0:1], 14, 1, op.bitwise_and, op.logical_shift_right))
+    V(v.tensor_scalar(T.jo[:], T.sp[:, 0:1], 1, None, op.bitwise_and))
+    V(v.tensor_scalar(T.jp[:], T.sp[:, 0:1], 16, 4, op.bitwise_and, op.logical_shift_right))
+    sync()
+    V(v.tensor_scalar(T.gap[:], T.sp2[:], 1.0 / STEP, -1.0, op.mult, op.add))
+    V(v.tensor_scalar(T.slot[:], T.pg[:], float(K // 16), float(K), op.mult, op.add))
+    V(v.tensor_tensor(T.jx[:], T.jo[:], T.jp[:], op.not_equal))
+    V(v.tensor_scalar(T.jt[:], T.jo[:], float(NB), None, op.add))
+    sync()
+    V(v.tensor_scalar(T.val[:], places(B - K, B), T.slot[:], None, op.add))
+    V(v.tensor_tensor(T.jm[:], T.jx[:], T.jt[:], op.mult))
+    v.wait_ge(S.lb, 16)
+    v.quantize_mx(T.win[:, 0:B], T.pln[:, 0:B], T.bt[:]).then_inc(S.qb, 1)
+    sync()
+    V(v.tensor_tensor(T.js[:], T.jm[:], T.jb[:], op.add))
+    v.wait_ge(S.lw, 16)
+    v.quantize_mx(T.wq[:, 0:256], T.wp[:, 0:256], T.wt[:, 0:1024]).then_inc(S.qw, 1)
+    sync()
+    V(v.tensor_scalar(T.sel[:, 0:1], T.js[:], float(2 * NB), None, op.min))
+
+    def last_w():
+        v.wait_ge(S.lw2, 16)
+        v.quantize_mx(T.wq[:, 256:384], T.wp[:, 256:384], T.wt[:, 1024:1536]).then_inc(S.qw2, 1)
+
+    if not first:
+        last_w()
+    v.wait_ge(S.ll, 16)
+    V(v.tensor_tensor(T.lf[:], T.li[:], T.gap[:], op.max))
+    sync()
+    V(v.tensor_scalar(T.lo[:], T.lf[:], float(STEP), float(STEP), op.mult, op.add))
+    sync()
+    V(v.tensor_copy(T.tb[:, W0:W0 + STEP * (B + 1)].indirect(T.lo[:, 0:4]), T.val[:]))
+    sync()
+    V(v.transpose(T.tt[:, 0:B], places(0, B)))
+    V(v.transpose(T.tt[:, B:2 * B + 32], places(-LEAD, B + LEAD)))
+    sync()
+    W = 2 * B + 32
+    V(v.tensor_tensor(T.ee[:], T.tt[:, 0:W:32], T.tt[:, 16:W:32], op.max))
+    sync()
+    src = T.ee
+    if rank >= 4:
+        V(v.tensor_tensor(T.u2[:], src[0:64, :], src[64:128, :], op.max))
+        sync()
+        src = T.u2
+    for q in range(4):
+        o = T.u3[32 * q:32 * q + 32, :]
+        if rank >= 2:
+            V(v.tensor_tensor(o, src[0:32, :], src[32:64, :], op.max))
+        else:
+            V(v.tensor_copy(o, src[0:32, :]))
+    sync()
+    v.tensor_copy(T.off[:], T.u3[:].indirect(T.sel[:, 0:1])).then_inc(S.of, 1)
+    v.wait_ge(S.of, 1)
+    v.wait_ge(S.qx, 1)
+    v.wait_ge(S.qb, 1)
+    for w in ("f0c", "f1c", "rc"):
+        if w in want:
+            v.wait_ge(S[w], want[w])
+    v.tensor_copy(T.mq[:].bitcast(dt.uint32), T.win[:, 0:full].bitcast(dt.uint32).indirect(T.off[:, 0:B // 16])).then_inc(S.pk, 1)
+    if first:
+        last_w()
+    v.wait_ge(S.mm0, 1)
+    v.tensor_copy(T.ysb[:, 0:B], T.acc[:, 0:B]).then_inc(S.yc0, 1)
+    v.wait_ge(S.mm2, 1)
+    v.tensor_copy(T.ysb[:, 2 * B:3 * B], T.acc[:, 1024:1024 + B]).then_inc(S.yc2, 1)
+
+    h = g.scalar
+    h.wait_ge(S.of, 1)
+    h.wait_ge(S.qx, 1)
+    h.wait_ge(S.qb, 1)
+    for w in ("fp", "rp"):
+        if w in want:
+            h.wait_ge(S[w], want[w])
+    h.activation(T.mp[:], T.pln[:, 0:full].indirect(T.off[:, 0:B // 16]), Copy).then_inc(S.ps, 1)
+    h.wait_ge(S.mm1, 1)
+    h.activation(T.ysb[:, B:2 * B], T.acc[:, 512:512 + B], Copy).then_inc(S.yc1, 1)
+    h.wait_ge(S.yc1, 1)
+    h.dma_start(T.y[:, B:2 * B], T.ysb[:, B:2 * B]).then_inc(S.sy1, 16)
+
+    t = g.tensor
+    t.wait_ge(S.qw, 1)
+    t.wait_ge(S.pk, 1)
+    t.wait_ge(S.ps, 1)
+    for o in range(O):
+        w0, w1 = 128 * o, 128 * o + 128
+        if o == 2:
+            t.wait_ge(S.qw2, 1)
+        t.matmul_mx(T.acc[:, 512 * o:512 * o + B], T.wq[:, w0:w1], T.wp[:, w0:w1], T.mq[:], T.mp[:], True, True).then_inc(S["mm%d" % o], 1)
+
+    y = g.sync
+    y.wait_ge(S.lm, 1)
+    y.wait_ge(S.lp, 32)
+    if lists:
+        y.wait_ge(S.ls, lists)
+    y.dma_start(T.li[0:16 * (rank + 1), :], T.L[0:rank + 1, 0:K, :]).then_inc(S.ll, 16)
+    y.wait_ge(S.yc0, 1)
+    y.dma_start(T.y[:, 0:B], T.ysb[:, 0:B]).then_inc(S.sy0, 16)
+    y.wait_ge(S.yc2, 1)
+    y.dma_start(T.y[:, 2 * B:3 * B], T.ysb[:, 2 * B:3 * B]).then_inc(S.sy2, 16)
+    y.wait_ge(S.sy0, 16)
+    y.wait_ge(S.sy1, 16)
+    y.wait_ge(S.sy2, 16)
+    v.wait_ge(S.vv, nv[0])

@@ -1,13 +1,11 @@
 from concourse.bass import DstId, RemoteDMATransfer
-from concourse.mybir import dt, AluOpType, ActivationFunctionType
+from concourse.mybir import dt, AluOpType, ActivationFunctionType, AxisListType
 
 B, K, O, N = 192, 64, 3, 8
-LEAD = 16
-STEP = K
-PL = LEAD + B + LEAD
-W0 = STEP * LEAD
-TAB = STEP * PL + 1
-NB = B // 32
+Q = B // 4
+STEP = K // 2
+AT0 = 3 * Q + 1
+TAB = STEP * (AT0 + B - 1) + 1
 WIN = B + K * (N + 1)
 SCRATCH = {
     "xt": ("sbuf", [128, 8 * K], "bfloat16"),
@@ -21,33 +19,38 @@ SCRATCH = {
     "mp": ("sbuf", [128, B], "uint8"),
     "ysb": ("sbuf", [128, O * B], "float32"),
     "acc": ("psum", [128, 512 * O], "float32"),
-    "L": ("dram", [N, 128, 1], "int32"),
-    "li": ("sbuf", [128, 4], "int32"),
-    "lf": ("sbuf", [128, 4], "float32"),
-    "lo": ("sbuf", [128, 4], "uint16"),
-    "sp": ("sbuf", [128, 4], "int32"),
-    "sp2": ("sbuf", [128, 4], "int32"),
-    "gap": ("sbuf", [128, 4], "float32"),
-    "pg": ("sbuf", [128, 1], "int32"),
-    "slot": ("sbuf", [128, 1], "float32"),
-    "jb": ("sbuf", [128, 1], "int32"),
-    "jo": ("sbuf", [128, 1], "int32"),
-    "jp": ("sbuf", [128, 1], "int32"),
-    "jx": ("sbuf", [128, 1], "int32"),
-    "jt": ("sbuf", [128, 1], "int32"),
-    "jm": ("sbuf", [128, 1], "int32"),
-    "js": ("sbuf", [128, 1], "int32"),
-    "sel": ("sbuf", [128, 2], "uint16"),
-    "val": ("sbuf", [128, K], "float32"),
+    "li": ("sbuf", [128, 2], "int32"),
+    "lf": ("sbuf", [128, 2], "float32"),
+    "lo": ("sbuf", [128, 2], "uint16"),
+    "sp": ("sbuf", [128, 2], "int32"),
+    "sp2": ("sbuf", [128, 2], "int32"),
+    "gap": ("sbuf", [128, 2], "float32"),
+    "pq": ("sbuf", [128, 1], "int32"),
+    "ph": ("sbuf", [128, 1], "int32"),
+    "shift": ("sbuf", [128, 1], "float32"),
+    "base": ("sbuf", [128, 1], "float32"),
+    "half": ("sbuf", [128, 1], "float32"),
+    "ramp": ("sbuf", [128, 80], "float32"),
+    "row": ("sbuf", [128, K // 2], "float32"),
+    "val": ("sbuf", [128, K // 2], "float32"),
     "tb": ("sbuf", [128, TAB], "float32"),
-    "tt": ("sbuf", [128, 32 * (2 * NB + 1)], "float32"),
-    "ee": ("sbuf", [128, 2 * NB + 1], "float32"),
-    "u2": ("sbuf", [64, 2 * NB + 1], "float32"),
-    "u3": ("sbuf", [128, 2 * NB + 1], "float32"),
+    "tt": ("sbuf", [128, 128], "float32"),
+    "tabs": ("sbuf", [128, 8 * N], "float16"),
+    "jj": ("sbuf", [128, 1], "int32"),
+    "jh": ("sbuf", [128, 1], "int32"),
+    "jq": ("sbuf", [128, 1], "int32"),
+    "j3": ("sbuf", [128, 1], "int32"),
+    "jf": ("sbuf", [128, 1], "float32"),
+    "jg": ("sbuf", [128, 1], "float32"),
+    "js": ("sbuf", [128, 1], "int32"),
+    "jm": ("sbuf", [128, 1], "int32"),
+    "sel": ("sbuf", [128, 2], "uint16"),
+    "u": ("sbuf", [128, 16], "float32"),
     "off": ("sbuf", [128, 16], "uint16"),
 }
-SEMAPHORES = ["lx", "lp", "lb", "lw", "lw2", "ll", "sy0", "sy1", "sy2", "lm", "it", "vv", "qx", "qb", "qw", "qw2", "of",
-              "pk", "ps", "mm0", "mm1", "mm2", "yc0", "yc1", "yc2", "go", "sent", "ls", "f0c", "f1c", "fp", "rc", "rp"]
+SEMAPHORES = ["lx", "lp", "lb", "lw", "lw2", "sy0", "sy1", "sy2", "it", "it2", "kb", "ks", "vv", "qx", "tq", "qb", "qw",
+              "qw2", "of", "pk", "ps", "mm0", "mm1", "mm2", "yc0", "yc1", "yc2", "go", "sent", "ls", "f0c", "f1c", "fp",
+              "rc", "rp", "r1", "r2", "r3", "xc", "xp"]
 
 
 def bits(es):
@@ -68,7 +71,7 @@ def plan(T, topo):
             chips.append([r])
     home = [c for c in chips if topo.host(C[c[0]]) == low]
     away = [c for c in chips if c not in home]
-    calls, lists = {}, {}
+    calls = {}
     for s in range(N):
         mine = [c for c in chips if s in c][0]
         far = [r for r in range(N) if r not in mine]
@@ -77,27 +80,39 @@ def plan(T, topo):
         stay = [e for e in topo.engines(C[s], C[mate]) if e not in out]
         near = [r for r in far if r > s and topo.host(C[r]) == topo.host(C[s])]
         up = [mate] if mate > s else []
-        if s < N - 1:
-            lists[s] = (out[:1], list(range(N - 1, s, -1)))
+        above = [r for r in reversed(far) if r > s]
         calls[s] = []
 
-        def slot(parts):
-            for what in ("c", "p"):
-                calls[s].append((s, 1, what, [], [(es, rs, sem[what]) for es, rs, sem in parts]))
+        def add(what, parts):
+            parts = [(es, rs, sem[what]) for es, rs, sem in parts if rs]
+            if parts:
+                calls[s].append((s, 1, what, [], parts))
 
-        rsem = {"c": "rc", "p": "rp"}
+        rsem = {"c": "rc", "p": "rp", "t": "ls"}
         if mine in home:
             cross = sorted([c[0] for c in away], key=lambda r: not topo.same_plane(C[s], C[r]))
-            slot([(out, cross, {"c": "f%dc" % home.index(mine), "p": "fp"})])
+            csem = {"c": "f%dc" % home.index(mine), "p": "fp"}
+            add("c", [(out, cross, csem)])
             if near:
-                slot([(out, near, rsem)] + ([(stay[:4], up, rsem)] if up else []))
-            elif up:
-                slot([(out, up, rsem)])
+                xsem = {"c": "xc", "p": "xp", "t": "ls"}
+                i = mine.index(s)
+                add("p", [(stay, [mate], xsem)])
+                add("c", [(stay, [mate], xsem)])
+                add("t", [(out, [r for r in above if r not in near], rsem), (stay, up, rsem)])
+                calls[s].append((mine[0], len(mine), "p", ["xp"], [(out, [cross[i]], "fp")]))
+                add("t", [(out, near, rsem)])
+                for what in "cp":
+                    calls[s].append((mine[0], len(mine), what, [xsem[what]], [(out, [near[i]], rsem[what])]))
+            else:
+                add("c", [(stay, up, rsem)])
+                add("t", [(out, above, rsem), (stay, up, rsem)])
+                add("p", [(out, cross, csem), (stay, up, rsem)])
         else:
-            if near:
-                slot([(out, near, rsem)] + ([(stay, up, rsem)] if up else []))
-            elif up:
-                slot([(out + stay, up, rsem)])
+            for what in "ctp":
+                if near:
+                    add(what, [(out, near, rsem), (stay, up, rsem)])
+                else:
+                    add(what, [(out + stay, up, rsem)])
             if up:
                 for c in sorted(home, key=lambda c: not topo.same_plane(C[s], C[c[0]])):
                     calls[s].append((c[0], len(c), "c", ["f%dc" % home.index(c)], [(out + stay, up, "rc")]))
@@ -108,7 +123,7 @@ def plan(T, topo):
             for es, rs, sem in tr:
                 for r in rs:
                     want[r][sem] = want[r].get(sem, 0) + len(es)
-    return calls, lists, want, low
+    return calls, want, low
 
 
 def rank_program(g, core, T, topo):
@@ -116,52 +131,54 @@ def rank_program(g, core, T, topo):
     if rank is None:
         return
     C = T.cores
-    calls, nlist, wants, low = plan(T, topo)
+    calls, wants, low = plan(T, topo)
     want = wants[rank]
-    first = topo.host(core) == low
     S = T.sem
     op = AluOpType
-    Copy = ActivationFunctionType.Copy
+    Copy, Identity = ActivationFunctionType.Copy, ActivationFunctionType.Identity
     a = B + K * rank
     full = B + K * (rank + 1)
-    lists = sum(len(nlist[s][0]) for s in nlist if rank in nlist[s][1])
 
     def dst(r):
         rid, pid = topo.addr(C[r], core)
         return DstId(rid=rid, pnc=pid)
 
-    g.scalar.dma_start(T.L[rank, 0:K, :], T.pl[:]).then_inc(S.lp, 16)
-    g.sync.dma_start(T.L[rank, K:2 * K, :], T.pl[:]).then_inc(S.lp, 16)
-    g.sync.dma_start(T.xt[:, 0:4 * K], T.x[:]).then_inc(S.lx, 16)
-    g.scalar.dma_start(T.bt[:], T.b[:]).then_inc(S.lb, 16)
-    g.scalar.dma_start(T.wt[:, 0:1024], T.w[:, 0:1024]).then_inc(S.lw, 16)
-    if first:
-        g.scalar.wait_ge(S.go, 1)
-    g.scalar.dma_start(T.wt[:, 1024:1536], T.w[:, 1024:1536]).then_inc(S.lw2, 16)
+    def places(l0, l1):
+        return T.tb[:, STEP * (AT0 + l0):STEP * (AT0 + l1 - 1) + 1:STEP]
 
-    g.iota(T.sp[:], [[16, 4]], 0, 1).then_inc(S.it, 1)
+    z = K if rank == 0 else 0
+    g.sync.dma_start(T.xt[:, 4 * z:4 * (z + K)], T.x[:]).then_inc(S.lx, 16)
+    for q in range(4):
+        (g.scalar if q < 2 else g.sync).dma_start(T.li[32 * q:32 * q + 32, :], T.pl[:]).then_inc(S.lp, 16)
+    h = g.scalar
+    g.sync.dma_start(T.bt[:], T.b[:]).then_inc(S.lb, 16)
+    g.sync.dma_start(T.wt[:], T.w[:]).then_inc(S.lw, 16)
+    h.wait_ge(S.it2, 2)
+    h.wait_ge(S.kb, 2)
+    h.activation(T.val[:], T.row[:], Identity, bias=T.half[:]).then_inc(S.ks, 1)
+    h.activation(places(-16, 64), T.ramp[:], Identity, bias=T.base[:]).then_inc(S.ks, 1)
+
+    g.iota(T.sp[:], [[16, 2]], 0, 1).then_inc(S.it, 1)
+    g.iota(T.row[:], [[16, 2], [1, 8], [32, 2]], a, 0, allow_small_or_imprecise_dtypes=True).then_inc(S.it2, 1)
+    g.iota(T.ramp[:], [[1, 80]], -16, 0, allow_small_or_imprecise_dtypes=True).then_inc(S.it2, 1)
     sent = 0
-    if rank in nlist:
-        es, rs = nlist[rank]
-        g.wait_ge(S.lp, 32)
-        g.remote_dma_fused([RemoteDMATransfer(dst_ids=[dst(r) for r in rs], dma_engine_mask=bits(es), remote_sem=S.ls,
-                                              srcs=[T.L[rank]], dsts=[T.L[rank] for r in rs])], local_sem=S.sent)
-        sent += len(es)
-    ready = False
+    waited = []
     for slot, n, what, waits, tr in calls[rank]:
         c0, c1 = B + K * slot, B + K * (slot + n)
-        if slot == rank and not ready:
-            g.wait_ge(S.qx, 1)
-            ready = True
+        own = "tq" if what == "t" else "qx"
+        if slot == rank and own not in waited:
+            g.wait_ge(S[own], 1)
+            waited.append(own)
         for w in waits:
             g.wait_ge(S[w], want[w])
-        view = T.win[:, c0:c1].bitcast(dt.uint8) if what == "c" else T.pln[:, c0:c1]
-        ts = [RemoteDMATransfer(dst_ids=[dst(r) for r in rs], dma_engine_mask=bits(es), remote_sem=S[sem],
-                                srcs=[view], dsts=[view for r in rs]) for es, rs, sem in tr]
+        if what == "t":
+            views = [T.tabs[:, 8 * s:8 * s + 4] for s in range(slot, slot + n)]
+        else:
+            views = [T.win[:, c0:c1].bitcast(dt.uint8) if what == "c" else T.pln[:, c0:c1]]
+        ts = [RemoteDMATransfer(dst_ids=[dst(r) for r in rs], dma_engine_mask=bits(es), remote_sem=S[sem], srcs=views,
+                                dsts=[views[-1] for r in rs], alu_op=2 if len(views) > 1 else 0) for es, rs, sem in tr]
         g.remote_dma_fused(ts, local_sem=S.sent)
         sent += sum(len(es) for es, rs, sem in tr)
-    if first:
-        g.sem_inc(S.go, 1)
     if sent:
         g.wait_ge(S.sent, sent)
 
@@ -174,98 +191,95 @@ def rank_program(g, core, T, topo):
     def sync():
         g.vector.wait_ge(S.vv, nv[0])
 
-    def places(l0, l1):
-        return T.tb[:, W0 + STEP * (l0 + 1):W0 + STEP * l1 + 1:STEP]
-
     v = g.vector
-    V(v.memset(T.xt[:, 4 * K:8 * K], 0.0))
-    v.memset(T.li[:], -1).then_inc(S.lm, 1)
-    V(v.memset(T.tt[:, 0:PL], 1.0))
-    sync()
-    V(v.tensor_tensor_scan(places(-LEAD, B + LEAD), T.tt[:, 0:PL], T.tt[:, 0:PL], float(-LEAD - 1), op.add, op.mult))
-    v.wait_ge(S.lx, 16)
-    v.quantize_mx(T.win[:, a:a + 2 * K], T.pln[:, a:a + 2 * K], T.xt[:]).then_inc(S.qx, 1)
+    p = T.sp[:, 0:1]
+    V(v.memset(T.xt[:, 4 * (K - z):4 * (2 * K - z)], 0.0))
     v.wait_ge(S.it, 1)
-    V(v.tensor_scalar(T.sp2[:], T.sp[:], K - 1, None, op.bitwise_and))
-    V(v.tensor_scalar(T.pg[:], T.sp[:, 0:1], 112, None, op.bitwise_and))
-    V(v.tensor_scalar(T.jb[:], T.sp[:, 0:1], 14, 1, op.bitwise_and, op.logical_shift_right))
-    V(v.tensor_scalar(T.jo[:], T.sp[:, 0:1], 1, None, op.bitwise_and))
-    V(v.tensor_scalar(T.jp[:], T.sp[:, 0:1], 16, 4, op.bitwise_and, op.logical_shift_right))
+    V(v.tensor_scalar(T.pq[:], p, 5, None, op.logical_shift_right))
+    V(v.tensor_scalar(T.ph[:], p, 1, 8, op.logical_shift_right, op.bitwise_and))
+    V(v.tensor_scalar(T.sp2[:], T.sp[:], STEP - 1, None, op.bitwise_and))
     sync()
+    v.tensor_scalar(T.base[:], T.pq[:], float(Q), None, op.mult).then_inc(S.kb, 1)
+    v.tensor_copy(T.half[:], T.ph[:]).then_inc(S.kb, 1)
     V(v.tensor_scalar(T.gap[:], T.sp2[:], 1.0 / STEP, -1.0, op.mult, op.add))
-    V(v.tensor_scalar(T.slot[:], T.pg[:], float(K // 16), float(K), op.mult, op.add))
-    V(v.tensor_tensor(T.jx[:], T.jo[:], T.jp[:], op.not_equal))
-    V(v.tensor_scalar(T.jt[:], T.jo[:], float(NB), None, op.add))
+    V(v.tensor_scalar(T.shift[:], T.pq[:], float(-STEP * Q), float(STEP * AT0), op.mult, op.add))
+    v.wait_ge(S.lx, 16)
+    v.quantize_mx(T.win[:, a - z:a - z + 2 * K], T.pln[:, a - z:a - z + 2 * K], T.xt[:]).then_inc(S.qx, 1)
+    v.wait_ge(S.lp, 64)
     sync()
-    V(v.tensor_scalar(T.val[:], places(B - K, B), T.slot[:], None, op.add))
-    V(v.tensor_tensor(T.jm[:], T.jx[:], T.jt[:], op.mult))
-    v.wait_ge(S.lb, 16)
-    v.quantize_mx(T.win[:, 0:B], T.pln[:, 0:B], T.bt[:]).then_inc(S.qb, 1)
-    sync()
-    V(v.tensor_tensor(T.js[:], T.jm[:], T.jb[:], op.add))
-    v.wait_ge(S.lw, 16)
-    v.quantize_mx(T.wq[:, 0:256], T.wp[:, 0:256], T.wt[:, 0:1024]).then_inc(S.qw, 1)
-    sync()
-    V(v.tensor_scalar(T.sel[:, 0:1], T.js[:], float(2 * NB), None, op.min))
-
-    def last_w():
-        v.wait_ge(S.lw2, 16)
-        v.quantize_mx(T.wq[:, 256:384], T.wp[:, 256:384], T.wt[:, 1024:1536]).then_inc(S.qw2, 1)
-
-    if not first:
-        last_w()
-    v.wait_ge(S.ll, 16)
     V(v.tensor_tensor(T.lf[:], T.li[:], T.gap[:], op.max))
     sync()
-    V(v.tensor_scalar(T.lo[:], T.lf[:], float(STEP), float(STEP), op.mult, op.add))
+    V(v.tensor_scalar(T.lo[:], T.lf[:], float(STEP), T.shift[:], op.mult, op.add))
     sync()
-    V(v.tensor_copy(T.tb[:, W0:W0 + STEP * (B + 1)].indirect(T.lo[:, 0:4]), T.val[:]))
+    v.wait_ge(S.ks, 2)
+    V(v.tensor_copy(T.tb[:].indirect(T.lo[:]), T.val[:]))
     sync()
-    V(v.transpose(T.tt[:, 0:B], places(0, B)))
-    V(v.transpose(T.tt[:, B:2 * B + 32], places(-LEAD, B + LEAD)))
+    V(v.transpose(T.tt[:, 0:64], places(0, 64)))
+    V(v.transpose(T.tt[:, 64:128], places(-16, 48)))
     sync()
-    W = 2 * B + 32
-    V(v.tensor_tensor(T.ee[:], T.tt[:, 0:W:32], T.tt[:, 16:W:32], op.max))
+    v.tensor_tensor(T.tabs[:, 8 * rank:8 * rank + 4], T.tt[:, 0:128:32], T.tt[:, 16:128:32], op.max).then_inc(S.tq, 1)
+    V(v.tensor_scalar(T.jj[:], p, 15, None, op.bitwise_and))
+    V(v.tensor_scalar(T.jh[:], p, 4, 1, op.logical_shift_right, op.bitwise_and))
+    V(v.tensor_scalar(T.jq[:], p, 3, 12, op.logical_shift_right, op.bitwise_and))
+    v.wait_ge(S.lb, 16)
+    v.wait_ge(S.qx, 1)
+    v.quantize_mx(T.win[:, 0:B], T.pln[:, 0:B], T.bt[:]).then_inc(S.qb, 1)
     sync()
-    src = T.ee
-    if rank >= 4:
-        V(v.tensor_tensor(T.u2[:], src[0:64, :], src[64:128, :], op.max))
-        sync()
-        src = T.u2
+    V(v.tensor_scalar(T.j3[:], T.jj[:], 1.0 / 3, 17 - 1.0 / 3, op.mult, op.add))
+    V(v.tensor_copy(T.jf[:], T.jj[:]))
+    V(v.tensor_tensor(T.jg[:], T.jh[:], T.jq[:], op.add))
+    sync()
+    V(v.tensor_scalar(T.js[:], T.j3[:], T.jf[:], T.jg[:], op.add, op.subtract))
+    sync()
+    V(v.tensor_scalar(T.jm[:], T.js[:], 15, None, op.bitwise_and))
+    sync()
+    V(v.tensor_copy(T.sel[:, 0:1], T.jm[:]))
+    v.wait_ge(S.lw, 16)
+    v.quantize_mx(T.wq[:], T.wp[:], T.wt[:]).then_inc(S.qw, 1)
+    sync()
+    v.wait_ge(S.tq, 1)
+    if rank > 0:
+        v.wait_ge(S.ls, want["ls"])
+    lowest = min([rank] + [slot + n - 1 for s in range(rank) for slot, n, what, _, tr in calls[s]
+                           if what == "t" and any(rank in rs for _, rs, _ in tr)])
+    for x, m in enumerate((1, 3, 0, 2)):
+        v.tensor_reduce(T.u[:, m:m + 1], T.tabs[:, 8 * lowest + x:8 * rank + x + 1:8], AxisListType.X, op.max).then_inc(S.r1, 1)
+    v.wait_ge(S.r1, 4)
+    h.wait_ge(S.r1, 4)
     for q in range(4):
-        o = T.u3[32 * q:32 * q + 32, :]
-        if rank >= 2:
-            V(v.tensor_tensor(o, src[0:32, :], src[32:64, :], op.max))
-        else:
-            V(v.tensor_copy(o, src[0:32, :]))
-    sync()
-    v.tensor_copy(T.off[:], T.u3[:].indirect(T.sel[:, 0:1])).then_inc(S.of, 1)
+        n = (q + 1) % 4
+        o, i = T.u[32 * q:32 * q + 32, 4:8], T.u[32 * n:32 * n + 32, 0:4]
+        (v.tensor_copy(o, i) if q < 2 else h.activation(o, i, Copy)).then_inc(S.r2, 1)
+    v.wait_ge(S.r2, 4)
+    h.wait_ge(S.r2, 4)
+    v.tensor_copy(T.u[0:64, 8:16], T.u[64:128, 0:8]).then_inc(S.r3, 1)
+    h.activation(T.u[64:128, 8:16], T.u[0:64, 0:8], Copy).then_inc(S.r3, 1)
+    v.wait_ge(S.r3, 2)
+    v.tensor_copy(T.off[:], T.u[:].indirect(T.sel[:, 0:1])).then_inc(S.of, 1)
     v.wait_ge(S.of, 1)
     v.wait_ge(S.qx, 1)
     v.wait_ge(S.qb, 1)
-    for w in ("f0c", "f1c", "rc"):
+    for w in ("f0c", "f1c", "rc", "xc"):
         if w in want:
             v.wait_ge(S[w], want[w])
     v.tensor_copy(T.mq[:].bitcast(dt.uint32), T.win[:, 0:full].bitcast(dt.uint32).indirect(T.off[:, 0:B // 16])).then_inc(S.pk, 1)
-    if first:
-        last_w()
     v.wait_ge(S.mm0, 1)
     v.tensor_copy(T.ysb[:, 0:B], T.acc[:, 0:B]).then_inc(S.yc0, 1)
     v.wait_ge(S.mm2, 1)
     v.tensor_copy(T.ysb[:, 2 * B:3 * B], T.acc[:, 1024:1024 + B]).then_inc(S.yc2, 1)
 
-    h = g.scalar
     h.wait_ge(S.of, 1)
     h.wait_ge(S.qx, 1)
     h.wait_ge(S.qb, 1)
-    for w in ("fp", "rp"):
+    for w in ("fp", "rp", "xp"):
         if w in want:
             h.wait_ge(S[w], want[w])
     h.activation(T.mp[:], T.pln[:, 0:full].indirect(T.off[:, 0:B // 16]), Copy).then_inc(S.ps, 1)
     h.wait_ge(S.mm1, 1)
     h.activation(T.ysb[:, B:2 * B], T.acc[:, 512:512 + B], Copy).then_inc(S.yc1, 1)
     h.wait_ge(S.yc1, 1)
-    h.dma_start(T.y[:, B:2 * B], T.ysb[:, B:2 * B]).then_inc(S.sy1, 16)
+    h.wait_ge(S.yc2, 1)
+    h.dma_start(T.y[:, B:3 * B], T.ysb[:, B:3 * B]).then_inc(S.sy1, 16)
 
     t = g.tensor
     t.wait_ge(S.qw, 1)
@@ -273,21 +287,11 @@ def rank_program(g, core, T, topo):
     t.wait_ge(S.ps, 1)
     for o in range(O):
         w0, w1 = 128 * o, 128 * o + 128
-        if o == 2:
-            t.wait_ge(S.qw2, 1)
         t.matmul_mx(T.acc[:, 512 * o:512 * o + B], T.wq[:, w0:w1], T.wp[:, w0:w1], T.mq[:], T.mp[:], True, True).then_inc(S["mm%d" % o], 1)
 
     y = g.sync
-    y.wait_ge(S.lm, 1)
-    y.wait_ge(S.lp, 32)
-    if lists:
-        y.wait_ge(S.ls, lists)
-    y.dma_start(T.li[0:16 * (rank + 1), :], T.L[0:rank + 1, 0:K, :]).then_inc(S.ll, 16)
     y.wait_ge(S.yc0, 1)
     y.dma_start(T.y[:, 0:B], T.ysb[:, 0:B]).then_inc(S.sy0, 16)
-    y.wait_ge(S.yc2, 1)
-    y.dma_start(T.y[:, 2 * B:3 * B], T.ysb[:, 2 * B:3 * B]).then_inc(S.sy2, 16)
     y.wait_ge(S.sy0, 16)
     y.wait_ge(S.sy1, 16)
-    y.wait_ge(S.sy2, 16)
     v.wait_ge(S.vv, nv[0])

from concourse.bass import DstId, RemoteDMATransfer
from concourse.mybir import dt, AluOpType, ActivationFunctionType, AxisListType

B, K, O, N = 192, 64, 3, 8
Q = B // 4
STEP = K // 2
AT0 = 3 * Q + 1
TAB = STEP * (AT0 + B - 1) + 1
WIN = B + K * (N + 1)
SCRATCH = {
    "xt": ("sbuf", [128, 8 * K], "bfloat16"),
    "bt": ("sbuf", [128, 4 * B], "bfloat16"),
    "wt": ("sbuf", [128, 512 * O], "bfloat16"),
    "win": ("sbuf", [128, WIN], "float8_e4m3fn_x4"),
    "pln": ("sbuf", [128, WIN], "uint8"),
    "wq": ("sbuf", [128, 128 * O], "float8_e4m3fn_x4"),
    "wp": ("sbuf", [128, 128 * O], "uint8"),
    "mq": ("sbuf", [128, B], "float8_e4m3fn_x4"),
    "mp": ("sbuf", [128, B], "uint8"),
    "ysb": ("sbuf", [128, O * B], "float32"),
    "acc": ("psum", [128, 512 * O], "float32"),
    "li": ("sbuf", [128, 2], "int32"),
    "lf": ("sbuf", [128, 2], "float32"),
    "lo": ("sbuf", [128, 2], "uint16"),
    "sp": ("sbuf", [128, 2], "int32"),
    "sp2": ("sbuf", [128, 2], "int32"),
    "gap": ("sbuf", [128, 2], "float32"),
    "pq": ("sbuf", [128, 1], "int32"),
    "ph": ("sbuf", [128, 1], "int32"),
    "shift": ("sbuf", [128, 1], "float32"),
    "base": ("sbuf", [128, 1], "float32"),
    "half": ("sbuf", [128, 1], "float32"),
    "ramp": ("sbuf", [128, 80], "float32"),
    "row": ("sbuf", [128, K // 2], "float32"),
    "val": ("sbuf", [128, K // 2], "float32"),
    "tb": ("sbuf", [128, TAB], "float32"),
    "tt": ("sbuf", [128, 128], "float32"),
    "tabs": ("sbuf", [128, 8 * N], "float16"),
    "jj": ("sbuf", [128, 1], "int32"),
    "jh": ("sbuf", [128, 1], "int32"),
    "jq": ("sbuf", [128, 1], "int32"),
    "j3": ("sbuf", [128, 1], "int32"),
    "jf": ("sbuf", [128, 1], "float32"),
    "jg": ("sbuf", [128, 1], "float32"),
    "js": ("sbuf", [128, 1], "int32"),
    "jm": ("sbuf", [128, 1], "int32"),
    "sel": ("sbuf", [128, 2], "uint16"),
    "u": ("sbuf", [128, 16], "float32"),
    "off": ("sbuf", [128, 16], "uint16"),
}
SEMAPHORES = ["lx", "lp", "lb", "lw", "lw2", "sy0", "sy1", "sy2", "it", "it2", "kb", "ks", "vv", "qx", "tq", "qb", "qw",
              "qw2", "of", "pk", "ps", "mm0", "mm1", "mm2", "yc0", "yc1", "yc2", "go", "sent", "ls", "f0c", "f1c", "fp",
              "rc", "rp", "r1", "r2", "r3", "xc", "xp"]


def bits(es):
    m = 0
    for e in es:
        m |= 1 << e
    return m


def plan(T, topo):
    C = T.cores
    low = topo.host(C[0])
    chips = []
    for r in range(N):
        if chips and C[r] in topo.cores_of(C[chips[-1][0]]):
            chips[-1].append(r)
        else:
            chips.append([r])
    home = [c for c in chips if topo.host(C[c[0]]) == low]
    away = [c for c in chips if c not in home]
    calls = {}
    for s in range(N):
        mine = [c for c in chips if s in c][0]
        far = [r for r in range(N) if r not in mine]
        out = topo.engines(C[s], C[far[0]])
        mate = [r for r in mine if r != s][0]
        stay = [e for e in topo.engines(C[s], C[mate]) if e not in out]
        near = [r for r in far if r > s and topo.host(C[r]) == topo.host(C[s])]
        up = [mate] if mate > s else []
        above = [r for r in reversed(far) if r > s]
        calls[s] = []

        def add(what, parts):
            parts = [(es, rs, sem[what]) for es, rs, sem in parts if rs]
            if parts:
                calls[s].append((s, 1, what, [], parts))

        rsem = {"c": "rc", "p": "rp", "t": "ls"}
        if mine in home:
            cross = sorted([c[0] for c in away], key=lambda r: not topo.same_plane(C[s], C[r]))
            csem = {"c": "f%dc" % home.index(mine), "p": "fp"}
            add("c", [(out, cross, csem)])
            if near:
                xsem = {"c": "xc", "p": "xp", "t": "ls"}
                i = mine.index(s)
                add("p", [(stay, [mate], xsem)])
                add("c", [(stay, [mate], xsem)])
                add("t", [(out, [r for r in above if r not in near], rsem), (stay, up, rsem)])
                calls[s].append((mine[0], len(mine), "p", ["xp"], [(out, [cross[i]], "fp")]))
                add("t", [(out, near, rsem)])
                for what in "cp":
                    calls[s].append((mine[0], len(mine), what, [xsem[what]], [(out, [near[i]], rsem[what])]))
            else:
                add("c", [(stay, up, rsem)])
                add("t", [(out, above, rsem), (stay, up, rsem)])
                add("p", [(out, cross, csem), (stay, up, rsem)])
        else:
            for what in "ctp":
                if near:
                    add(what, [(out, near, rsem), (stay, up, rsem)])
                else:
                    add(what, [(out + stay, up, rsem)])
            if up:
                for c in sorted(home, key=lambda c: not topo.same_plane(C[s], C[c[0]])):
                    calls[s].append((c[0], len(c), "c", ["f%dc" % home.index(c)], [(out + stay, up, "rc")]))
                calls[s].append((home[0][0], sum(len(c) for c in home), "p", ["fp"], [(out + stay, up, "rp")]))
    want = {r: {} for r in range(N)}
    for s in range(N):
        for _, _, _, _, tr in calls[s]:
            for es, rs, sem in tr:
                for r in rs:
                    want[r][sem] = want[r].get(sem, 0) + len(es)
    return calls, want, low


def rank_program(g, core, T, topo):
    rank = T.rank_of(core)
    if rank is None:
        return
    C = T.cores
    calls, wants, low = plan(T, topo)
    want = wants[rank]
    S = T.sem
    op = AluOpType
    Copy, Identity = ActivationFunctionType.Copy, ActivationFunctionType.Identity
    a = B + K * rank
    full = B + K * (rank + 1)

    def dst(r):
        rid, pid = topo.addr(C[r], core)
        return DstId(rid=rid, pnc=pid)

    def places(l0, l1):
        return T.tb[:, STEP * (AT0 + l0):STEP * (AT0 + l1 - 1) + 1:STEP]

    z = K if rank == 0 else 0
    g.sync.dma_start(T.xt[:, 4 * z:4 * (z + K)], T.x[:]).then_inc(S.lx, 16)
    for q in range(4):
        (g.scalar if q < 2 else g.sync).dma_start(T.li[32 * q:32 * q + 32, :], T.pl[:]).then_inc(S.lp, 16)
    h = g.scalar
    g.sync.dma_start(T.bt[:], T.b[:]).then_inc(S.lb, 16)
    g.sync.dma_start(T.wt[:], T.w[:]).then_inc(S.lw, 16)
    h.wait_ge(S.it2, 2)
    h.wait_ge(S.kb, 2)
    h.activation(T.val[:], T.row[:], Identity, bias=T.half[:]).then_inc(S.ks, 1)
    h.activation(places(-16, 64), T.ramp[:], Identity, bias=T.base[:]).then_inc(S.ks, 1)

    g.iota(T.sp[:], [[16, 2]], 0, 1).then_inc(S.it, 1)
    g.iota(T.row[:], [[16, 2], [1, 8], [32, 2]], a, 0, allow_small_or_imprecise_dtypes=True).then_inc(S.it2, 1)
    g.iota(T.ramp[:], [[1, 80]], -16, 0, allow_small_or_imprecise_dtypes=True).then_inc(S.it2, 1)
    sent = 0
    waited = []
    for slot, n, what, waits, tr in calls[rank]:
        c0, c1 = B + K * slot, B + K * (slot + n)
        own = "tq" if what == "t" else "qx"
        if slot == rank and own not in waited:
            g.wait_ge(S[own], 1)
            waited.append(own)
        for w in waits:
            g.wait_ge(S[w], want[w])
        if what == "t":
            views = [T.tabs[:, 8 * s:8 * s + 4] for s in range(slot, slot + n)]
        else:
            views = [T.win[:, c0:c1].bitcast(dt.uint8) if what == "c" else T.pln[:, c0:c1]]
        ts = [RemoteDMATransfer(dst_ids=[dst(r) for r in rs], dma_engine_mask=bits(es), remote_sem=S[sem], srcs=views,
                                dsts=[views[-1] for r in rs], alu_op=2 if len(views) > 1 else 0) for es, rs, sem in tr]
        g.remote_dma_fused(ts, local_sem=S.sent)
        sent += sum(len(es) for es, rs, sem in tr)
    if sent:
        g.wait_ge(S.sent, sent)

    nv = [0]

    def V(ins):
        ins.then_inc(S.vv, 1)
        nv[0] += 1

    def sync():
        g.vector.wait_ge(S.vv, nv[0])

    v = g.vector
    p = T.sp[:, 0:1]
    V(v.memset(T.xt[:, 4 * (K - z):4 * (2 * K - z)], 0.0))
    v.wait_ge(S.it, 1)
    V(v.tensor_scalar(T.pq[:], p, 5, None, op.logical_shift_right))
    V(v.tensor_scalar(T.ph[:], p, 1, 8, op.logical_shift_right, op.bitwise_and))
    V(v.tensor_scalar(T.sp2[:], T.sp[:], STEP - 1, None, op.bitwise_and))
    sync()
    v.tensor_scalar(T.base[:], T.pq[:], float(Q), None, op.mult).then_inc(S.kb, 1)
    v.tensor_copy(T.half[:], T.ph[:]).then_inc(S.kb, 1)
    V(v.tensor_scalar(T.gap[:], T.sp2[:], 1.0 / STEP, -1.0, op.mult, op.add))
    V(v.tensor_scalar(T.shift[:], T.pq[:], float(-STEP * Q), float(STEP * AT0), op.mult, op.add))
    v.wait_ge(S.lx, 16)
    v.quantize_mx(T.win[:, a - z:a - z + 2 * K], T.pln[:, a - z:a - z + 2 * K], T.xt[:]).then_inc(S.qx, 1)
    v.wait_ge(S.lp, 64)
    sync()
    V(v.tensor_tensor(T.lf[:], T.li[:], T.gap[:], op.max))
    sync()
    V(v.tensor_scalar(T.lo[:], T.lf[:], float(STEP), T.shift[:], op.mult, op.add))
    sync()
    v.wait_ge(S.ks, 2)
    V(v.tensor_copy(T.tb[:].indirect(T.lo[:]), T.val[:]))
    sync()
    V(v.transpose(T.tt[:, 0:64], places(0, 64)))
    V(v.transpose(T.tt[:, 64:128], places(-16, 48)))
    sync()
    v.tensor_tensor(T.tabs[:, 8 * rank:8 * rank + 4], T.tt[:, 0:128:32], T.tt[:, 16:128:32], op.max).then_inc(S.tq, 1)
    V(v.tensor_scalar(T.jj[:], p, 15, None, op.bitwise_and))
    V(v.tensor_scalar(T.jh[:], p, 4, 1, op.logical_shift_right, op.bitwise_and))
    V(v.tensor_scalar(T.jq[:], p, 3, 12, op.logical_shift_right, op.bitwise_and))
    v.wait_ge(S.lb, 16)
    v.wait_ge(S.qx, 1)
    v.quantize_mx(T.win[:, 0:B], T.pln[:, 0:B], T.bt[:]).then_inc(S.qb, 1)
    sync()
    V(v.tensor_scalar(T.j3[:], T.jj[:], 1.0 / 3, 17 - 1.0 / 3, op.mult, op.add))
    V(v.tensor_copy(T.jf[:], T.jj[:]))
    V(v.tensor_tensor(T.jg[:], T.jh[:], T.jq[:], op.add))
    sync()
    V(v.tensor_scalar(T.js[:], T.j3[:], T.jf[:], T.jg[:], op.add, op.subtract))
    sync()
    V(v.tensor_scalar(T.jm[:], T.js[:], 15, None, op.bitwise_and))
    sync()
    V(v.tensor_copy(T.sel[:, 0:1], T.jm[:]))
    v.wait_ge(S.lw, 16)
    v.quantize_mx(T.wq[:], T.wp[:], T.wt[:]).then_inc(S.qw, 1)
    sync()
    v.wait_ge(S.tq, 1)
    if rank > 0:
        v.wait_ge(S.ls, want["ls"])
    lowest = min([rank] + [slot + n - 1 for s in range(rank) for slot, n, what, _, tr in calls[s]
                           if what == "t" and any(rank in rs for _, rs, _ in tr)])
    for x, m in enumerate((1, 3, 0, 2)):
        v.tensor_reduce(T.u[:, m:m + 1], T.tabs[:, 8 * lowest + x:8 * rank + x + 1:8], AxisListType.X, op.max).then_inc(S.r1, 1)
    v.wait_ge(S.r1, 4)
    h.wait_ge(S.r1, 4)
    for q in range(4):
        n = (q + 1) % 4
        o, i = T.u[32 * q:32 * q + 32, 4:8], T.u[32 * n:32 * n + 32, 0:4]
        (v.tensor_copy(o, i) if q < 2 else h.activation(o, i, Copy)).then_inc(S.r2, 1)
    v.wait_ge(S.r2, 4)
    h.wait_ge(S.r2, 4)
    v.tensor_copy(T.u[0:64, 8:16], T.u[64:128, 0:8]).then_inc(S.r3, 1)
    h.activation(T.u[64:128, 8:16], T.u[0:64, 0:8], Copy).then_inc(S.r3, 1)
    v.wait_ge(S.r3, 2)
    v.tensor_copy(T.off[:], T.u[:].indirect(T.sel[:, 0:1])).then_inc(S.of, 1)
    v.wait_ge(S.of, 1)
    v.wait_ge(S.qx, 1)
    v.wait_ge(S.qb, 1)
    for w in ("f0c", "f1c", "rc", "xc"):
        if w in want:
            v.wait_ge(S[w], want[w])
    v.tensor_copy(T.mq[:].bitcast(dt.uint32), T.win[:, 0:full].bitcast(dt.uint32).indirect(T.off[:, 0:B // 16])).then_inc(S.pk, 1)
    v.wait_ge(S.mm0, 1)
    v.tensor_copy(T.ysb[:, 0:B], T.acc[:, 0:B]).then_inc(S.yc0, 1)
    v.wait_ge(S.mm2, 1)
    v.tensor_copy(T.ysb[:, 2 * B:3 * B], T.acc[:, 1024:1024 + B]).then_inc(S.yc2, 1)

    h.wait_ge(S.of, 1)
    h.wait_ge(S.qx, 1)
    h.wait_ge(S.qb, 1)
    for w in ("fp", "rp", "xp"):
        if w in want:
            h.wait_ge(S[w], want[w])
    h.activation(T.mp[:], T.pln[:, 0:full].indirect(T.off[:, 0:B // 16]), Copy).then_inc(S.ps, 1)
    h.wait_ge(S.mm1, 1)
    h.activation(T.ysb[:, B:2 * B], T.acc[:, 512:512 + B], Copy).then_inc(S.yc1, 1)
    h.wait_ge(S.yc1, 1)
    h.wait_ge(S.yc2, 1)
    h.dma_start(T.y[:, B:3 * B], T.ysb[:, B:3 * B]).then_inc(S.sy1, 16)

    t = g.tensor
    t.wait_ge(S.qw, 1)
    t.wait_ge(S.pk, 1)
    t.wait_ge(S.ps, 1)
    for o in range(O):
        w0, w1 = 128 * o, 128 * o + 128
        t.matmul_mx(T.acc[:, 512 * o:512 * o + B], T.wq[:, w0:w1], T.wp[:, w0:w1], T.mq[:], T.mp[:], True, True).then_inc(S["mm%d" % o], 1)

    y = g.sync
    y.wait_ge(S.yc0, 1)
    y.dma_start(T.y[:, 0:B], T.ysb[:, 0:B]).then_inc(S.sy0, 16)
    y.wait_ge(S.sy0, 16)
    y.wait_ge(S.sy1, 16)
    v.wait_ge(S.vv, nv[0])
